import numpy as np
import ml_dtypes


def mxq(x, axis, fmt="e4m3"):
    dtype, down = {"e4m3": (ml_dtypes.float8_e4m3fn, 7), "e5m2": (ml_dtypes.float8_e5m2, 14)}[fmt]
    v = np.moveaxis(np.asarray(x, np.float32).astype(ml_dtypes.bfloat16).astype(np.float64), axis, -1)
    blocks = v.reshape(v.shape[:-1] + (-1, 32))
    amax = np.abs(blocks).max(-1, keepdims=True)
    byte = np.maximum(np.where(amax > 0, np.frexp(amax)[1] - 1 + 127, 0) - down, 1)
    scale = np.exp2(byte - 127.0)
    codes = (blocks / scale).astype(np.float32).astype(dtype).astype(np.float64)
    return np.moveaxis((codes * scale).reshape(v.shape), -1, axis)


WIDE = False


def mx_kscale(k):
    if not WIDE:
        return np.ones(k)
    levels = np.array([10, -10, 5, -5, 0])
    if k % 512:
        return np.exp2(np.random.permutation(np.resize(levels, k // 32))).repeat(32)
    a = np.empty((k // 512, 16))
    for p in range(k // 512):
        a[p, :8] = np.random.permutation(np.resize(levels, 8))
        for g in range(8):
            far = levels[np.abs(levels - a[p, g]) >= 10]
            a[p, g + 8] = far[np.random.randint(len(far))]
    return np.exp2(a.ravel()).repeat(32)


def f64(x):
    return np.asarray(x).astype(np.float64)


def striped(idx):
    return np.tile(idx.reshape(-1, 16).T, (8, 1)).astype(np.uint16)


def unstriped(offs):
    return offs[:16].T.reshape(-1).astype(np.int64)


def pack_weight(w):
    k, n = w.shape
    w = f64(np.asarray(w, np.float32).astype(ml_dtypes.bfloat16)).reshape(k // 32, 32, n)
    amax = np.abs(w).max(1)
    byte = np.clip(np.where(amax > 0, np.frexp(amax)[1] - 1 + 127 - 7, 1), 1, 254)
    scaled = (w * np.exp2(127.0 - byte)[:, None, :]).reshape(k, n).astype(np.float32)
    words = np.ascontiguousarray(scaled.reshape(k // 512, 128, 4, n).transpose(0, 1, 3, 2)).astype(ml_dtypes.float8_e4m3fn).view(np.uint8)
    return words, np.ascontiguousarray(byte.astype(np.uint8).reshape(k // 512, 16, n))


def unpack_weight(words, scales):
    g, p, n, _ = words.shape
    vals = np.ascontiguousarray(words).view(ml_dtypes.float8_e4m3fn).astype(np.float64) * np.repeat(np.exp2(scales.astype(np.float64) - 127.0), 8, axis=1)[..., None]
    return vals.transpose(0, 1, 3, 2).reshape(g * 512, n)


K, T, S, V, U = 512, 1024, 512, 256, 256


def setup_inputs():
    n = np.random.standard_normal
    s = mx_kscale(K)[:, None]
    packed_xT = pack_weight(n((K, T)) * s)
    return {
        "x_words": packed_xT[0],
        "x_scales": packed_xT[1],
        "h0": (n((K, V)) / np.sqrt(K) / s).astype(np.float32),
        "h1": (n((K, V)) / np.sqrt(K) / s).astype(np.float32),
        "h2": (n((K, V)) / np.sqrt(K) / s).astype(np.float32),
        "offs": striped(np.random.permutation(T)[:S]),
        "tree1": striped(np.random.randint(0, S, U)),
        "tree2": striped(np.random.randint(0, S, U)),
        "tree3": striped(np.random.randint(0, S, U)),
    }


def reference(x_words, x_scales, h0, h1, h2, offs, tree1, tree2, tree3):
    h0q = mxq(f64(h0), 0, "e4m3")
    xq = unpack_weight(x_words, x_scales)[:, unstriped(offs)]
    y0 = h0q.T @ xq
    e0 = np.exp(y0)
    s0 = np.log(e0.sum(axis=1, keepdims=True))
    l0 = y0 - s0
    h1q = mxq(f64(h1), 0, "e4m3")
    y1 = h1q.T @ xq
    e1 = np.exp(y1)
    s1 = np.log(e1.sum(axis=1, keepdims=True))
    l1 = y1 - s1
    h2q = mxq(f64(h2), 0, "e4m3")
    y2 = h2q.T @ xq
    e2 = np.exp(y2)
    s2 = np.log(e2.sum(axis=1, keepdims=True))
    l2 = y2 - s2
    return np.exp((l0[:, unstriped(tree1)] + l1[:, unstriped(tree2)] + l2[:, unstriped(tree3)]) / 3)

@@ -1,0 +1,167 @@
+from contextlib import ExitStack
+
+import concourse.mybir as mybir
+
+K, T, S, V, U = 512, 1024, 512, 256, 256
+FLOPS = 3 * 2 * K * V * S
+
+F32 = mybir.dt.float32
+BF16 = mybir.dt.bfloat16
+I32 = mybir.dt.int32
+U32 = mybir.dt.uint32
+U16 = mybir.dt.uint16
+U8 = mybir.dt.uint8
+FP8X4 = mybir.dt.float8_e4m3fn_x4
+ALU = mybir.AluOpType
+ACT = mybir.ActivationFunctionType
+
+P = 128
+PACK = 4
+HEADS = 3
+BLOCKS = V // P
+HALF = S // 2
+
+
+def tile_picked_ymedu_mean_p_kernel(
+    tc, x_words, x_scales, h0, h1, h2, offs, tree1, tree2, tree3, out
+):
+    nc = tc.nc
+    with ExitStack() as ctx:
+        lists = ctx.enter_context(tc.tile_pool(name="lists", bufs=1))
+        sb = ctx.enter_context(tc.tile_pool(name="sb", bufs=1))
+        psum = ctx.enter_context(tc.psum_pool(name="psum", bufs=1))
+
+        table_scales = sb.tile([P, T], U8, name="table_scales", align_bytes=64)
+        nc.vector.memset(table_scales[:].bitcast(I32), 0)
+        for q in range(4):
+            nc.scalar.dma_start(
+                out=table_scales[32 * q : 32 * q + 4, :].bitcast(I32),
+                in_=x_scales[0, 4 * q : 4 * q + 4, :].bitcast(I32),
+            )
+
+        picks = lists.tile([P, S // 16], U16, name="picks")
+        nc.sync.dma_start(picks[:], offs)
+        table_words = sb.tile([P, T], U32, name="table_words", align_bytes=64)
+        nc.sync.dma_start(
+            out=table_words[:].bitcast(I32),
+            in_=x_words[0].rearrange("p n t -> p (n t)").bitcast(I32),
+        )
+        raw = [sb.tile([P, PACK, V], F32, name="raw%d" % h, tag="raw%d" % h) for h in range(HEADS)]
+        paths = [lists.tile([P, U // 16], U16, name="path%d" % h) for h in range(HEADS)]
+        hidden = [states.rearrange("(p j) w -> p j w", j=PACK) for states in (h0, h1, h2)]
+        nc.sync.dma_start(out=raw[0][:], in_=hidden[0])
+        nc.sync.dma_start(paths[0][:], tree1)
+        nc.sync.dma_start(out=raw[1][:], in_=hidden[1])
+        nc.sync.dma_start(out=raw[2][:], in_=hidden[2])
+        nc.sync.dma_start(paths[1][:], tree2)
+        nc.sync.dma_start(paths[2][:], tree3)
+
+        minus_one = sb.tile([P, 1], F32, name="minus_one")
+        nc.vector.memset(minus_one[:], -1.0)
+        minus_third = sb.tile([P, 1], F32, name="minus_third")
+        nc.scalar.activation(minus_third[:], minus_one[:], ACT.Identity, scale=1.0 / HEADS)
+
+        x_codes = sb.tile([P, S], U32, name="x_codes", align_bytes=64)
+        nc.vector.tensor_copy(x_codes[:], table_words[:].indirect(picks[:]))
+        x_bytes = sb.tile([P, S], U8, name="x_bytes", align_bytes=64)
+
+        def pick_bytes(half):
+            nc.vector.tensor_copy(
+                x_bytes[:, half * HALF : (half + 1) * HALF],
+                table_scales[:].indirect(picks[:, half * HALF // 16 : (half + 1) * HALF // 16]),
+            )
+
+        units = [(h, b) for h in range(HEADS) for b in range(BLOCKS)]
+        grouped, codes, planes, banks, scores = {}, {}, {}, {}, {}
+        neg_max = [sb.tile([P, HEADS], F32, name="neg_max%d" % b) for b in range(BLOCKS)]
+        sums = [sb.tile([P, HEADS], F32, name="sums%d" % b) for b in range(BLOCKS)]
+        picked = {}
+
+        def cast(u):
+            h, b = u
+            grouped[u] = sb.tile([P, P, PACK], BF16, name="grouped%d%d" % u, align_bytes=64)
+            nc.scalar.copy(
+                grouped[u][:].rearrange("p (c i) t -> p c t i", i=4),
+                raw[h][:, :, b * P : (b + 1) * P].rearrange("p t (c i) -> p c t i", i=4),
+            )
+
+        def quantise(u):
+            codes[u] = sb.tile([P, P], U32, name="codes%d%d" % u, align_bytes=64)
+            planes[u] = sb.tile([P, P], U8, name="plane%d%d" % u, align_bytes=64)
+            nc.vector.quantize_mx(
+                out=codes[u][:].bitcast(FP8X4),
+                scales=planes[u][:],
+                in_=grouped[u][:].rearrange("p w j -> p (w j)"),
+            )
+
+        def multiply(u, width=S):
+            banks[u] = psum.tile([P, S], F32, name="bank%d%d" % u)
+            for c in range(0, S, width):
+                nc.tensor.matmul_mx(
+                    out=banks[u][:, c : c + width],
+                    lhsT=codes[u][:].bitcast(FP8X4),
+                    lhsT_scale=planes[u][:],
+                    rhs=x_codes[:, c : c + width].bitcast(FP8X4),
+                    rhs_scale=x_bytes[:, c : c + width],
+                    start=True,
+                    stop=True,
+                )
+
+        def leave_psum(u):
+            h, b = u
+            scores[u] = sb.tile([P, S], F32, name="scores%d%d" % u)
+            nc.vector.tensor_scalar(
+                scores[u][:], banks[u][:], -1.0, None, ALU.mult, ALU.min,
+                accum_out=neg_max[b][:, h : h + 1],
+            )
+
+        def sum_exp(u):
+            h, b = u
+            nc.scalar.activation(
+                spent[:, h * BLOCKS + b, :], scores[u][:], ACT.Exp, bias=neg_max[b][:, h : h + 1], scale=-1.0,
+                accum_out=sums[b][:, h : h + 1],
+            )
+
+        def fetch(u):
+            h, b = u
+            picked[u] = sb.tile([P, U], F32, name="picked%d%d" % u)
+            window = scores[u][:].indirect(paths[h][:])
+            if h == 0:
+                nc.vector.tensor_copy(picked[u][:], window)
+            else:
+                nc.vector.tensor_tensor(picked[u][:], window, picked[h - 1, b][:], ALU.add)
+
+        def finish(b):
+            pair = sb.tile([P, 1], F32, name="pair%d" % b)
+            nc.gpsimd.tensor_tensor(pair[:], sums[b][:, 0:1], sums[b][:, 1:2], ALU.mult)
+            root_pair = sb.tile([P, 1], F32, name="root_pair%d" % b)
+            nc.gpsimd.tensor_tensor(root_pair[:], pair[:], minus_third[:], ALU.pow)
+            root_last = sb.tile([P, 1], F32, name="root_last%d" % b)
+            nc.gpsimd.tensor_tensor(root_last[:], sums[b][:, 2:3], minus_third[:], ALU.pow)
+            thirds = sb.tile([P, HEADS], F32, name="thirds%d" % b)
+            shift = sb.tile([P, 1], F32, name="shift%d" % b)
+            nc.scalar.activation(thirds[:], neg_max[b][:], ACT.Identity, scale=1.0 / HEADS, accum_out=shift[:])
+            mean = sb.tile([P, U], F32, name="mean%d" % b)
+            nc.scalar.activation(mean[:], picked[HEADS - 1, b][:], ACT.Exp, bias=shift[:], scale=-1.0 / HEADS)
+            result = sb.tile([P, U], F32, name="result%d" % b)
+            nc.vector.tensor_scalar(result[:], mean[:], root_pair[:], root_last[:], ALU.mult, ALU.mult)
+            nc.sync.dma_start(out=out[b * P : (b + 1) * P, :], in_=result[:])
+
+        for u in units:
+            cast(u)
+        pick_bytes(0)
+        quantise(units[0])
+        pick_bytes(1)
+        multiply(units[0], HALF)
+        for u in units[1:]:
+            quantise(u)
+            multiply(u)
+        spent = sb.tile([P, len(units), S], BF16, name="spent", tag="raw2")
+        for i, u in enumerate(units):
+            leave_psum(u)
+            sum_exp(u)
+            if i > 0:
+                fetch(units[i - 1])
+        finish(0)
+        fetch(units[-1])
+        finish(1)

@@ -20,6 +20,7 @@ PACK = 4
 HEADS = 3
 BLOCKS = V // P
 HALF = S // 2
+RAW_BYTES = 4 * PACK * V
 
 
 def tile_picked_ymedu_mean_p_kernel(
@@ -28,140 +29,156 @@ def tile_picked_ymedu_mean_p_kernel(
     nc = tc.nc
     with ExitStack() as ctx:
         lists = ctx.enter_context(tc.tile_pool(name="lists", bufs=1))
+        reused = ctx.enter_context(tc.tile_pool(name="reused", bufs=1))
         sb = ctx.enter_context(tc.tile_pool(name="sb", bufs=1))
         psum = ctx.enter_context(tc.psum_pool(name="psum", bufs=1))
 
         table_scales = sb.tile([P, T], U8, name="table_scales", align_bytes=64)
         nc.vector.memset(table_scales[:].bitcast(I32), 0)
+        picks = lists.tile([P, S // 16], U16, name="picks")
+        nc.sync.dma_start(picks[:], offs)
         for q in range(4):
-            nc.scalar.dma_start(
+            nc.sync.dma_start(
                 out=table_scales[32 * q : 32 * q + 4, :].bitcast(I32),
                 in_=x_scales[0, 4 * q : 4 * q + 4, :].bitcast(I32),
             )
 
-        picks = lists.tile([P, S // 16], U16, name="picks")
-        nc.sync.dma_start(picks[:], offs)
+        pieces = [(0, 0, P), (0, P, P), (1, 0, V), (2, 0, V)]
+        raw = []
+
+        def load(i):
+            h, first, width = pieces[i]
+            raw.append(reused.tile([P, PACK, width], F32, name="raw%d" % i, offset=i * RAW_BYTES))
+            states = (h0, h1, h2)[h].rearrange("(p j) w -> p j w", j=PACK)
+            nc.sync.dma_start(out=raw[i][:], in_=states[:, :, first : first + width])
+
+        load(0)
         table_words = sb.tile([P, T], U32, name="table_words", align_bytes=64)
         nc.sync.dma_start(
             out=table_words[:].bitcast(I32),
             in_=x_words[0].rearrange("p n t -> p (n t)").bitcast(I32),
         )
-        raw = [sb.tile([P, PACK, V], F32, name="raw%d" % h, tag="raw%d" % h) for h in range(HEADS)]
-        paths = [lists.tile([P, U // 16], U16, name="path%d" % h) for h in range(HEADS)]
-        hidden = [states.rearrange("(p j) w -> p j w", j=PACK) for states in (h0, h1, h2)]
-        nc.sync.dma_start(out=raw[0][:], in_=hidden[0])
-        nc.sync.dma_start(paths[0][:], tree1)
-        nc.sync.dma_start(out=raw[1][:], in_=hidden[1])
-        nc.sync.dma_start(out=raw[2][:], in_=hidden[2])
-        nc.sync.dma_start(paths[1][:], tree2)
-        nc.sync.dma_start(paths[2][:], tree3)
+        for i in range(1, len(pieces)):
+            load(i)
+        paths = []
+        for h, tree in enumerate((tree1, tree2, tree3)):
+            paths.append(lists.tile([P, U // 16], U16, name="path%d" % h))
+            nc.sync.dma_start(paths[h][:], tree)
 
-        minus_one = sb.tile([P, 1], F32, name="minus_one")
+        minus_one = sb.tile([P, 2], F32, name="minus_one")
         nc.vector.memset(minus_one[:], -1.0)
-        minus_third = sb.tile([P, 1], F32, name="minus_third")
+        minus_third = sb.tile([P, 2], F32, name="minus_third")
         nc.scalar.activation(minus_third[:], minus_one[:], ACT.Identity, scale=1.0 / HEADS)
 
-        x_codes = sb.tile([P, S], U32, name="x_codes", align_bytes=64)
-        nc.vector.tensor_copy(x_codes[:], table_words[:].indirect(picks[:]))
         x_bytes = sb.tile([P, S], U8, name="x_bytes", align_bytes=64)
+        nc.vector.tensor_copy(x_bytes[:], table_scales[:].indirect(picks[:]))
 
-        def pick_bytes(half):
-            nc.vector.tensor_copy(
-                x_bytes[:, half * HALF : (half + 1) * HALF],
-                table_scales[:].indirect(picks[:, half * HALF // 16 : (half + 1) * HALF // 16]),
-            )
-
-        units = [(h, b) for h in range(HEADS) for b in range(BLOCKS)]
-        grouped, codes, planes, banks, scores = {}, {}, {}, {}, {}
-        neg_max = [sb.tile([P, HEADS], F32, name="neg_max%d" % b) for b in range(BLOCKS)]
-        sums = [sb.tile([P, HEADS], F32, name="sums%d" % b) for b in range(BLOCKS)]
-        picked = {}
-
-        def cast(u):
-            h, b = u
-            grouped[u] = sb.tile([P, P, PACK], BF16, name="grouped%d%d" % u, align_bytes=64)
+        grouped = []
+        for i, (h, first, width) in enumerate(pieces):
+            grouped.append(sb.tile([P, width, PACK], BF16, name="grouped%d" % i, align_bytes=64))
             nc.scalar.copy(
-                grouped[u][:].rearrange("p (c i) t -> p c t i", i=4),
-                raw[h][:, :, b * P : (b + 1) * P].rearrange("p t (c i) -> p c t i", i=4),
+                grouped[i][:].rearrange("p (c n) j -> p c j n", n=4),
+                raw[i][:].rearrange("p j (c n) -> p c j n", n=4),
             )
 
-        def quantise(u):
-            codes[u] = sb.tile([P, P], U32, name="codes%d%d" % u, align_bytes=64)
-            planes[u] = sb.tile([P, P], U8, name="plane%d%d" % u, align_bytes=64)
+        h_codes, h_bytes, banks = {}, {}, {}
+
+        def quantise(i):
+            h, first, width = pieces[i]
+            codes = sb.tile([P, width], U32, name="h_codes%d" % i, align_bytes=64)
+            plane = sb.tile([P, width], U8, name="h_bytes%d" % i, align_bytes=64)
             nc.vector.quantize_mx(
-                out=codes[u][:].bitcast(FP8X4),
-                scales=planes[u][:],
-                in_=grouped[u][:].rearrange("p w j -> p (w j)"),
+                out=codes[:].bitcast(FP8X4), scales=plane[:], in_=grouped[i][:].rearrange("p w j -> p (w j)")
             )
+            for c in range(0, width, P):
+                h_codes[h, (first + c) // P] = codes[:, c : c + P]
+                h_bytes[h, (first + c) // P] = plane[:, c : c + P]
 
-        def multiply(u, width=S):
+        def multiply(u, width):
             banks[u] = psum.tile([P, S], F32, name="bank%d%d" % u)
             for c in range(0, S, width):
                 nc.tensor.matmul_mx(
                     out=banks[u][:, c : c + width],
-                    lhsT=codes[u][:].bitcast(FP8X4),
-                    lhsT_scale=planes[u][:],
+                    lhsT=h_codes[u].bitcast(FP8X4),
+                    lhsT_scale=h_bytes[u],
                     rhs=x_codes[:, c : c + width].bitcast(FP8X4),
                     rhs_scale=x_bytes[:, c : c + width],
                     start=True,
                     stop=True,
                 )
 
-        def leave_psum(u):
-            h, b = u
-            scores[u] = sb.tile([P, S], F32, name="scores%d%d" % u)
-            nc.vector.tensor_scalar(
-                scores[u][:], banks[u][:], -1.0, None, ALU.mult, ALU.min,
-                accum_out=neg_max[b][:, h : h + 1],
+        units = [(h, b) for h in range(HEADS) for b in range(BLOCKS)]
+        quantise(0)
+        x_codes = sb.tile([P, S], U32, name="x_codes", align_bytes=64)
+        for c in range(0, S, HALF):
+            nc.vector.tensor_copy(
+                x_codes[:, c : c + HALF], table_words[:].indirect(picks[:, c // 16 : (c + HALF) // 16])
             )
-
-        def sum_exp(u):
-            h, b = u
-            nc.scalar.activation(
-                spent[:, h * BLOCKS + b, :], scores[u][:], ACT.Exp, bias=neg_max[b][:, h : h + 1], scale=-1.0,
-                accum_out=sums[b][:, h : h + 1],
-            )
-
-        def fetch(u):
-            h, b = u
-            picked[u] = sb.tile([P, U], F32, name="picked%d%d" % u)
-            window = scores[u][:].indirect(paths[h][:])
-            if h == 0:
-                nc.vector.tensor_copy(picked[u][:], window)
-            else:
-                nc.vector.tensor_tensor(picked[u][:], window, picked[h - 1, b][:], ALU.add)
-
-        def finish(b):
-            pair = sb.tile([P, 1], F32, name="pair%d" % b)
-            nc.gpsimd.tensor_tensor(pair[:], sums[b][:, 0:1], sums[b][:, 1:2], ALU.mult)
-            root_pair = sb.tile([P, 1], F32, name="root_pair%d" % b)
-            nc.gpsimd.tensor_tensor(root_pair[:], pair[:], minus_third[:], ALU.pow)
-            root_last = sb.tile([P, 1], F32, name="root_last%d" % b)
-            nc.gpsimd.tensor_tensor(root_last[:], sums[b][:, 2:3], minus_third[:], ALU.pow)
-            thirds = sb.tile([P, HEADS], F32, name="thirds%d" % b)
-            shift = sb.tile([P, 1], F32, name="shift%d" % b)
-            nc.scalar.activation(thirds[:], neg_max[b][:], ACT.Identity, scale=1.0 / HEADS, accum_out=shift[:])
-            mean = sb.tile([P, U], F32, name="mean%d" % b)
-            nc.scalar.activation(mean[:], picked[HEADS - 1, b][:], ACT.Exp, bias=shift[:], scale=-1.0 / HEADS)
-            result = sb.tile([P, U], F32, name="result%d" % b)
-            nc.vector.tensor_scalar(result[:], mean[:], root_pair[:], root_last[:], ALU.mult, ALU.mult)
-            nc.sync.dma_start(out=out[b * P : (b + 1) * P, :], in_=result[:])
-
-        for u in units:
-            cast(u)
-        pick_bytes(0)
-        quantise(units[0])
-        pick_bytes(1)
         multiply(units[0], HALF)
+        for i in range(1, len(pieces)):
+            quantise(i)
         for u in units[1:]:
-            quantise(u)
-            multiply(u)
-        spent = sb.tile([P, len(units), S], BF16, name="spent", tag="raw2")
-        for i, u in enumerate(units):
-            leave_psum(u)
-            sum_exp(u)
+            multiply(u, S)
+
+        neg_max = [sb.tile([P, HEADS], F32, name="neg_max%d" % b) for b in range(BLOCKS)]
+        sums = [sb.tile([P, 2], F32, name="sums%d" % b) for b in range(BLOCKS)]
+        factors = [sb.tile([P, 2], F32, name="factors%d" % b) for b in range(BLOCKS)]
+        spent = reused.tile([P, len(units), S], BF16, name="spent", offset=3 * RAW_BYTES + 4 * S)
+        neg_scores, neg_total, roots, shift = {}, {}, {}, {}
+
+        def leave_psum(i):
+            h, b = u = units[i]
+            if i + 1 < len(pieces):
+                neg_scores[u] = reused.tile([P, S], F32, name="neg_scores%d" % i, offset=(i + 1) * RAW_BYTES)
+            else:
+                neg_scores[u] = sb.tile([P, S], F32, name="neg_scores%d" % i)
+            nc.vector.tensor_scalar(
+                neg_scores[u][:], banks[u][:], -1.0, None, ALU.mult, ALU.min, accum_out=neg_max[b][:, h : h + 1]
+            )
+
+        def normalise(i):
+            h, b = u = units[i]
+            total = factors[b][:, 1:2] if h == HEADS - 1 else sums[b][:, h : h + 1]
+            nc.scalar.activation(
+                spent[:, i, :], neg_scores[u][:], ACT.Exp, bias=neg_max[b][:, h : h + 1], scale=-1.0, accum_out=total
+            )
+            if h == 1:
+                nc.scalar.activation(factors[b][:, 0:1], sums[b][:, 0:1], ACT.Identity, scale=sums[b][:, 1:2])
+            if h == HEADS - 1:
+                roots[b] = sb.tile([P, 2], F32, name="roots%d" % b)
+                nc.gpsimd.tensor_tensor(roots[b][:], factors[b][:], minus_third[:], ALU.pow)
+                thirds = sb.tile([P, HEADS], F32, name="thirds%d" % b)
+                shift[b] = sb.tile([P, 1], F32, name="shift%d" % b)
+                nc.scalar.activation(
+                    thirds[:], neg_max[b][:], ACT.Identity, scale=1.0 / HEADS, accum_out=shift[b][:]
+                )
+
+        def fetch(i):
+            h, b = u = units[i]
+            neg_total[u] = sb.tile([P, U], F32, name="neg_total%d" % i)
+            width = U // 2 if i == len(units) - 1 else U
+            spans = [slice(c, c + width) for c in range(0, U, width)]
+            for span in spans:
+                window = neg_scores[u][:].indirect(paths[h][:, span.start // 16 : span.stop // 16])
+                if h == 0:
+                    nc.vector.tensor_copy(neg_total[u][:, span], window)
+                else:
+                    nc.vector.tensor_tensor(neg_total[u][:, span], window, neg_total[h - 1, b][:, span], ALU.add)
+            if h == HEADS - 1:
+                mean = sb.tile([P, U], F32, name="mean%d" % b)
+                result = sb.tile([P, U], F32, name="result%d" % b)
+                for span in spans:
+                    nc.scalar.activation(
+                        mean[:, span], neg_total[u][:, span], ACT.Exp, bias=shift[b][:], scale=-1.0 / HEADS
+                    )
+                    nc.vector.tensor_scalar(
+                        result[:, span], mean[:, span], roots[b][:, 0:1], roots[b][:, 1:2], ALU.mult, ALU.mult
+                    )
+                    nc.sync.dma_start(out=out[b * P : (b + 1) * P, span], in_=result[:, span])
+
+        for i in range(len(units)):
+            leave_psum(i)
+            normalise(i)
             if i > 0:
-                fetch(units[i - 1])
-        finish(0)
-        fetch(units[-1])
-        finish(1)
+                fetch(i - 1)
+        fetch(len(units) - 1)

@@ -20,7 +20,7 @@ PACK = 4
 HEADS = 3
 BLOCKS = V // P
 HALF = S // 2
-RAW_BYTES = 4 * PACK * V
+KIB = 1024
 
 
 def tile_picked_ymedu_mean_p_kernel(
@@ -33,33 +33,33 @@ def tile_picked_ymedu_mean_p_kernel(
         sb = ctx.enter_context(tc.tile_pool(name="sb", bufs=1))
         psum = ctx.enter_context(tc.psum_pool(name="psum", bufs=1))
 
+        states = [h.rearrange("(p j) w -> p j w", j=PACK) for h in (h0, h1, h2)]
+        raw0 = [reused.tile([P, PACK, P], F32, name="raw0%d" % b, offset=2 * KIB * b) for b in range(BLOCKS)]
+        raw1 = reused.tile([P, PACK, V], F32, name="raw1", offset=4 * KIB)
+        raw2 = reused.tile([P, PACK, V], F32, name="raw2", offset=8 * KIB)
+        raw = {(0, 0): raw0[0][:], (0, 1): raw0[1][:]}
+        for b in range(BLOCKS):
+            raw[1, b] = raw1[:, :, b * P : (b + 1) * P]
+            raw[2, b] = raw2[:, :, b * P : (b + 1) * P]
+
         table_scales = sb.tile([P, T], U8, name="table_scales", align_bytes=64)
         nc.vector.memset(table_scales[:].bitcast(I32), 0)
         picks = lists.tile([P, S // 16], U16, name="picks")
         nc.sync.dma_start(picks[:], offs)
-        for q in range(4):
-            nc.sync.dma_start(
-                out=table_scales[32 * q : 32 * q + 4, :].bitcast(I32),
-                in_=x_scales[0, 4 * q : 4 * q + 4, :].bitcast(I32),
-            )
-
-        pieces = [(0, 0, P), (0, P, P), (1, 0, V), (2, 0, V)]
-        raw = []
-
-        def load(i):
-            h, first, width = pieces[i]
-            raw.append(reused.tile([P, PACK, width], F32, name="raw%d" % i, offset=i * RAW_BYTES))
-            states = (h0, h1, h2)[h].rearrange("(p j) w -> p j w", j=PACK)
-            nc.sync.dma_start(out=raw[i][:], in_=states[:, :, first : first + width])
-
-        load(0)
         table_words = sb.tile([P, T], U32, name="table_words", align_bytes=64)
         nc.sync.dma_start(
             out=table_words[:].bitcast(I32),
             in_=x_words[0].rearrange("p n t -> p (n t)").bitcast(I32),
         )
-        for i in range(1, len(pieces)):
-            load(i)
+        for q in range(4):
+            nc.sync.dma_start(
+                out=table_scales[32 * q : 32 * q + 4, :].bitcast(I32),
+                in_=x_scales[0, 4 * q : 4 * q + 4, :].bitcast(I32),
+            )
+        for b in range(BLOCKS):
+            nc.sync.dma_start(out=raw0[b][:], in_=states[0][:, :, b * P : (b + 1) * P])
+        nc.sync.dma_start(out=raw1[:], in_=states[1])
+        nc.sync.dma_start(out=raw2[:], in_=states[2])
         paths = []
         for h, tree in enumerate((tree1, tree2, tree3)):
             paths.append(lists.tile([P, U // 16], U16, name="path%d" % h))
@@ -70,115 +70,157 @@ def tile_picked_ymedu_mean_p_kernel(
         minus_third = sb.tile([P, 2], F32, name="minus_third")
         nc.scalar.activation(minus_third[:], minus_one[:], ACT.Identity, scale=1.0 / HEADS)
 
-        x_bytes = sb.tile([P, S], U8, name="x_bytes", align_bytes=64)
-        nc.vector.tensor_copy(x_bytes[:], table_scales[:].indirect(picks[:]))
-
-        grouped = []
-        for i, (h, first, width) in enumerate(pieces):
-            grouped.append(sb.tile([P, width, PACK], BF16, name="grouped%d" % i, align_bytes=64))
-            nc.scalar.copy(
-                grouped[i][:].rearrange("p (c n) j -> p c j n", n=4),
-                raw[i][:].rearrange("p j (c n) -> p c j n", n=4),
-            )
-
-        h_codes, h_bytes, banks = {}, {}, {}
-
-        def quantise(i):
-            h, first, width = pieces[i]
-            codes = sb.tile([P, width], U32, name="h_codes%d" % i, align_bytes=64)
-            plane = sb.tile([P, width], U8, name="h_bytes%d" % i, align_bytes=64)
-            nc.vector.quantize_mx(
-                out=codes[:].bitcast(FP8X4), scales=plane[:], in_=grouped[i][:].rearrange("p w j -> p (w j)")
-            )
-            for c in range(0, width, P):
-                h_codes[h, (first + c) // P] = codes[:, c : c + P]
-                h_bytes[h, (first + c) // P] = plane[:, c : c + P]
-
-        def multiply(u, width):
-            banks[u] = psum.tile([P, S], F32, name="bank%d%d" % u)
-            for c in range(0, S, width):
-                nc.tensor.matmul_mx(
-                    out=banks[u][:, c : c + width],
-                    lhsT=h_codes[u].bitcast(FP8X4),
-                    lhsT_scale=h_bytes[u],
-                    rhs=x_codes[:, c : c + width].bitcast(FP8X4),
-                    rhs_scale=x_bytes[:, c : c + width],
-                    start=True,
-                    stop=True,
-                )
-
-        units = [(h, b) for h in range(HEADS) for b in range(BLOCKS)]
-        quantise(0)
         x_codes = sb.tile([P, S], U32, name="x_codes", align_bytes=64)
-        for c in range(0, S, HALF):
-            nc.vector.tensor_copy(
-                x_codes[:, c : c + HALF], table_words[:].indirect(picks[:, c // 16 : (c + HALF) // 16])
-            )
-        multiply(units[0], HALF)
-        for i in range(1, len(pieces)):
-            quantise(i)
-        for u in units[1:]:
-            multiply(u, S)
-
+        x_bytes = [
+            sb.tile([P, HALF], U8, name="x_bytes0", align_bytes=64),
+            reused.tile([P, HALF], U8, name="x_bytes1", offset=0, align_bytes=64),
+        ]
+        grouped, h_codes, h_bytes, banks = {}, {}, {}, {}
+        neg_scores, neg_total = {}, {}
         neg_max = [sb.tile([P, HEADS], F32, name="neg_max%d" % b) for b in range(BLOCKS)]
-        sums = [sb.tile([P, 2], F32, name="sums%d" % b) for b in range(BLOCKS)]
-        factors = [sb.tile([P, 2], F32, name="factors%d" % b) for b in range(BLOCKS)]
-        spent = reused.tile([P, len(units), S], BF16, name="spent", offset=3 * RAW_BYTES + 4 * S)
-        neg_scores, neg_total, roots, shift = {}, {}, {}, {}
+        neg_max_half = sb.tile([P, 1], F32, name="neg_max_half")
+        sums = [sb.tile([P, HEADS], F32, name="sums%d" % b) for b in range(BLOCKS)]
+        spent = {
+            (h, b): sb.tile([P, S], BF16, name="spent%d%d" % (h, b)) for h in range(HEADS) for b in range(BLOCKS)
+        }
+        spent[1, 1] = reused.tile([P, S], BF16, name="spent_late", offset=28 * KIB)
+        spent[2, 0] = reused.tile([P, S], BF16, name="spent_held", offset=26 * KIB - KIB // 2)
+        late = sb.tile([P, 2], F32, name="late")
+        total_offset = {(0, 0): 28 * KIB, (2, 0): 26 * KIB}
+        score_offset = {(0, 0): 4 * KIB, (0, 1): 22 * KIB, (1, 0): 8 * KIB, (2, 1): 24 * KIB}
 
-        def leave_psum(i):
-            h, b = u = units[i]
-            if i + 1 < len(pieces):
-                neg_scores[u] = reused.tile([P, S], F32, name="neg_scores%d" % i, offset=(i + 1) * RAW_BYTES)
+        def cast(dst, src, engine_copy):
+            engine_copy(dst.rearrange("p (c n) j -> p c j n", n=4), src.rearrange("p j (c n) -> p c j n", n=4))
+
+        def quantise(h, first, source):
+            width = source.shape[1]
+            codes = sb.tile([P, width], U32, name="h_codes%d%d" % (h, first), align_bytes=64)
+            plane = sb.tile([P, width], U8, name="h_bytes%d%d" % (h, first), align_bytes=64)
+            nc.vector.quantize_mx(
+                out=codes[:].bitcast(FP8X4), scales=plane[:], in_=source[:].rearrange("p w j -> p (w j)")
+            )
+            for b in range(width // P):
+                h_codes[h, first + b] = codes[:, b * P : (b + 1) * P]
+                h_bytes[h, first + b] = plane[:, b * P : (b + 1) * P]
+
+        def multiply(h, b, c, bank):
+            nc.tensor.matmul_mx(
+                out=bank,
+                lhsT=h_codes[h, b].bitcast(FP8X4),
+                lhsT_scale=h_bytes[h, b],
+                rhs=x_codes[:, c * HALF : (c + 1) * HALF].bitcast(FP8X4),
+                rhs_scale=x_bytes[c][:],
+                start=True,
+                stop=True,
+            )
+
+        def multiply_unit(h, b):
+            banks[h, b, 0] = psum.tile([P, S], F32, name="bank%d%d" % (h, b))
+            for c in range(2):
+                multiply(h, b, c, banks[h, b, 0][:, c * HALF : (c + 1) * HALF])
+
+        def scores(h, b):
+            if (h, b) in score_offset:
+                neg_scores[h, b] = reused.tile([P, S], F32, name="neg_scores%d%d" % (h, b), offset=score_offset[h, b])
             else:
-                neg_scores[u] = sb.tile([P, S], F32, name="neg_scores%d" % i)
+                neg_scores[h, b] = sb.tile([P, S], F32, name="neg_scores%d%d" % (h, b))
+            return neg_scores[h, b]
+
+        def leave_psum(h, b):
             nc.vector.tensor_scalar(
-                neg_scores[u][:], banks[u][:], -1.0, None, ALU.mult, ALU.min, accum_out=neg_max[b][:, h : h + 1]
+                scores(h, b)[:], banks[h, b, 0][:], -1.0, None, ALU.mult, ALU.min, accum_out=neg_max[b][:, h : h + 1]
             )
 
-        def normalise(i):
-            h, b = u = units[i]
-            total = factors[b][:, 1:2] if h == HEADS - 1 else sums[b][:, h : h + 1]
+        def row_sums(h, b):
+            unused = spent[h, b][:]
             nc.scalar.activation(
-                spent[:, i, :], neg_scores[u][:], ACT.Exp, bias=neg_max[b][:, h : h + 1], scale=-1.0, accum_out=total
+                unused, neg_scores[h, b][:], ACT.Exp, bias=neg_max[b][:, h : h + 1], scale=-1.0,
+                accum_out=late[:, 1:2] if (h, b) == (2, 1) else sums[b][:, h : h + 1],
             )
-            if h == 1:
-                nc.scalar.activation(factors[b][:, 0:1], sums[b][:, 0:1], ACT.Identity, scale=sums[b][:, 1:2])
-            if h == HEADS - 1:
-                roots[b] = sb.tile([P, 2], F32, name="roots%d" % b)
-                nc.gpsimd.tensor_tensor(roots[b][:], factors[b][:], minus_third[:], ALU.pow)
-                thirds = sb.tile([P, HEADS], F32, name="thirds%d" % b)
-                shift[b] = sb.tile([P, 1], F32, name="shift%d" % b)
-                nc.scalar.activation(
-                    thirds[:], neg_max[b][:], ACT.Identity, scale=1.0 / HEADS, accum_out=shift[b][:]
-                )
 
-        def fetch(i):
-            h, b = u = units[i]
-            neg_total[u] = sb.tile([P, U], F32, name="neg_total%d" % i)
-            width = U // 2 if i == len(units) - 1 else U
-            spans = [slice(c, c + width) for c in range(0, U, width)]
-            for span in spans:
-                window = neg_scores[u][:].indirect(paths[h][:, span.start // 16 : span.stop // 16])
-                if h == 0:
-                    nc.vector.tensor_copy(neg_total[u][:, span], window)
-                else:
-                    nc.vector.tensor_tensor(neg_total[u][:, span], window, neg_total[h - 1, b][:, span], ALU.add)
-            if h == HEADS - 1:
-                mean = sb.tile([P, U], F32, name="mean%d" % b)
-                result = sb.tile([P, U], F32, name="result%d" % b)
-                for span in spans:
-                    nc.scalar.activation(
-                        mean[:, span], neg_total[u][:, span], ACT.Exp, bias=shift[b][:], scale=-1.0 / HEADS
-                    )
-                    nc.vector.tensor_scalar(
-                        result[:, span], mean[:, span], roots[b][:, 0:1], roots[b][:, 1:2], ALU.mult, ALU.mult
-                    )
-                    nc.sync.dma_start(out=out[b * P : (b + 1) * P, span], in_=result[:, span])
+        def fetch(h, b):
+            window = neg_scores[h, b][:].indirect(paths[h][:])
+            if (h, b) in total_offset:
+                neg_total[h, b] = reused.tile([P, U], F32, name="neg_total%d%d" % (h, b), offset=total_offset[h, b])
+            else:
+                neg_total[h, b] = sb.tile([P, U], F32, name="neg_total%d%d" % (h, b))
+            if h == 0:
+                nc.scalar.activation(neg_total[h, b][:], window, ACT.Copy)
+            else:
+                nc.vector.tensor_tensor(neg_total[h, b][:], window, neg_total[h - 1, b][:], ALU.add)
 
-        for i in range(len(units)):
-            leave_psum(i)
-            normalise(i)
-            if i > 0:
-                fetch(i - 1)
-        fetch(len(units) - 1)
+        def row_shift(b):
+            thirds = sb.tile([P, HEADS], F32, name="thirds%d" % b)
+            total = sb.tile([P, 1], F32, name="shift%d" % b)
+            nc.scalar.activation(thirds[:], neg_max[b][:], ACT.Identity, scale=1.0 / HEADS, accum_out=total[:])
+            return total
+
+        def exp_mean(b):
+            mean = sb.tile([P, U], F32, name="mean%d" % b)
+            nc.scalar.activation(mean[:], neg_total[HEADS - 1, b][:], ACT.Exp, bias=shift[b][:], scale=-1.0 / HEADS)
+            return mean
+
+        halves = [picks[:, c * HALF // 16 : (c + 1) * HALF // 16] for c in range(2)]
+        nc.vector.tensor_copy(x_codes[:], table_words[:].indirect(picks[:]))
+        nc.vector.tensor_copy(x_bytes[0][:], table_scales[:].indirect(halves[0]))
+        for b in range(BLOCKS):
+            grouped[0, b] = sb.tile([P, P, PACK], BF16, name="grouped0%d" % b, align_bytes=64)
+            cast(grouped[0, b][:], raw[0, b], nc.scalar.copy)
+        quantise(0, 0, grouped[0, 0])
+        nc.vector.tensor_copy(x_bytes[1][:], table_scales[:].indirect(halves[1]))
+        for c in range(2):
+            banks[0, 0, c * HALF] = psum.tile([P, HALF], F32, name="bank00%d" % c)
+            multiply(0, 0, c, banks[0, 0, c * HALF][:])
+        quantise(0, 1, grouped[0, 1])
+        multiply_unit(0, 1)
+        grouped[1] = reused.tile([P, V, PACK], BF16, name="grouped1", offset=22 * KIB, align_bytes=64)
+        cast(grouped[1][:, 0:P, :], raw[1, 0], nc.scalar.copy)
+        cast(grouped[1][:, P:V, :], raw[1, 1], nc.vector.tensor_copy)
+        first = scores(0, 0)
+        nc.vector.tensor_scalar(
+            first[:, 0:HALF], banks[0, 0, 0][:], -1.0, None, ALU.mult, ALU.min, accum_out=neg_max_half[:]
+        )
+        quantise(1, 0, grouped[1])
+        for b in range(BLOCKS):
+            multiply_unit(1, b)
+        nc.vector.tensor_scalar(
+            first[:, HALF:S], banks[0, 0, HALF][:], -1.0, neg_max_half[:], ALU.mult, ALU.min,
+            accum_out=neg_max[0][:, 0:1],
+        )
+        leave_psum(0, 1)
+        for b in range(BLOCKS):
+            grouped[2, b] = sb.tile([P, P, PACK], BF16, name="grouped2%d" % b, align_bytes=64)
+            cast(grouped[2, b][:], raw[2, b], nc.scalar.copy)
+        for b in range(BLOCKS):
+            quantise(2, b, grouped[2, b])
+            multiply_unit(2, b)
+        leave_psum(1, 0)
+        row_sums(0, 0)
+        leave_psum(1, 1)
+        leave_psum(2, 0)
+        fetch(0, 0)
+        row_sums(1, 0)
+        fetch(0, 1)
+        row_sums(2, 0)
+        fetch(1, 0)
+        fetch(1, 1)
+        norm = sb.tile([P, 1], F32, name="norm")
+        root = [sb.tile([P, 1 + b], F32, name="root%d" % b) for b in range(BLOCKS)]
+        nc.vector.tensor_scalar(norm[:], sums[0][:, 0:1], sums[0][:, 1:2], sums[0][:, 2:3], ALU.mult, ALU.mult)
+        nc.gpsimd.tensor_tensor(root[0][:], norm[:], minus_third[:, 0:1], ALU.pow)
+        leave_psum(2, 1)
+        row_sums(0, 1)
+        row_sums(1, 1)
+        shift = [row_shift(0)]
+        nc.scalar.activation(late[:, 0:1], sums[1][:, 0:1], ACT.Identity, scale=sums[1][:, 1:2])
+        row_sums(2, 1)
+        shift.append(row_shift(1))
+        nc.gpsimd.tensor_tensor(root[1][:], late[:], minus_third[:], ALU.pow)
+        fetch(2, 0)
+        fetch(2, 1)
+        result = [sb.tile([P, U], F32, name="result%d" % b) for b in range(BLOCKS)]
+        means = [exp_mean(b) for b in range(BLOCKS)]
+        nc.scalar.activation(result[0][:], means[0][:], ACT.Identity, scale=root[0][:])
+        nc.sync.dma_start(out=out[0:P, :], in_=result[0][:])
+        nc.vector.tensor_scalar(result[1][:], means[1][:], root[1][:, 0:1], root[1][:, 1:2], ALU.mult, ALU.mult)
+        nc.sync.dma_start(out=out[P:V, :], in_=result[1][:])

@@ -34,32 +34,25 @@ def tile_picked_ymedu_mean_p_kernel(
         psum = ctx.enter_context(tc.psum_pool(name="psum", bufs=1))
 
         states = [h.rearrange("(p j) w -> p j w", j=PACK) for h in (h0, h1, h2)]
-        raw0 = [reused.tile([P, PACK, P], F32, name="raw0%d" % b, offset=2 * KIB * b) for b in range(BLOCKS)]
-        raw1 = reused.tile([P, PACK, V], F32, name="raw1", offset=4 * KIB)
-        raw2 = reused.tile([P, PACK, V], F32, name="raw2", offset=8 * KIB)
-        raw = {(0, 0): raw0[0][:], (0, 1): raw0[1][:]}
-        for b in range(BLOCKS):
-            raw[1, b] = raw1[:, :, b * P : (b + 1) * P]
-            raw[2, b] = raw2[:, :, b * P : (b + 1) * P]
+        raws = [reused.tile([P, PACK, V], F32, name="raw%d" % h, offset=4 * KIB * h) for h in range(HEADS)]
+        raw = {(h, b): raws[h][:, :, b * P : (b + 1) * P] for h in range(HEADS) for b in range(BLOCKS)}
 
         table_scales = sb.tile([P, T], U8, name="table_scales", align_bytes=64)
         nc.vector.memset(table_scales[:].bitcast(I32), 0)
-        picks = lists.tile([P, S // 16], U16, name="picks")
-        nc.sync.dma_start(picks[:], offs)
         table_words = sb.tile([P, T], U32, name="table_words", align_bytes=64)
         nc.sync.dma_start(
             out=table_words[:].bitcast(I32),
             in_=x_words[0].rearrange("p n t -> p (n t)").bitcast(I32),
         )
+        picks = lists.tile([P, S // 16], U16, name="picks")
+        nc.sync.dma_start(picks[:], offs)
         for q in range(4):
             nc.sync.dma_start(
                 out=table_scales[32 * q : 32 * q + 4, :].bitcast(I32),
                 in_=x_scales[0, 4 * q : 4 * q + 4, :].bitcast(I32),
             )
-        for b in range(BLOCKS):
-            nc.sync.dma_start(out=raw0[b][:], in_=states[0][:, :, b * P : (b + 1) * P])
-        nc.sync.dma_start(out=raw1[:], in_=states[1])
-        nc.sync.dma_start(out=raw2[:], in_=states[2])
+        for h in range(HEADS):
+            nc.sync.dma_start(out=raws[h][:], in_=states[h])
         paths = []
         for h, tree in enumerate((tree1, tree2, tree3)):
             paths.append(lists.tile([P, U // 16], U16, name="path%d" % h))
@@ -71,14 +64,10 @@ def tile_picked_ymedu_mean_p_kernel(
         nc.scalar.activation(minus_third[:], minus_one[:], ACT.Identity, scale=1.0 / HEADS)
 
         x_codes = sb.tile([P, S], U32, name="x_codes", align_bytes=64)
-        x_bytes = [
-            sb.tile([P, HALF], U8, name="x_bytes0", align_bytes=64),
-            reused.tile([P, HALF], U8, name="x_bytes1", offset=0, align_bytes=64),
-        ]
+        x_bytes = sb.tile([P, S], U8, name="x_bytes", align_bytes=64)
         grouped, h_codes, h_bytes, banks = {}, {}, {}, {}
         neg_scores, neg_total = {}, {}
         neg_max = [sb.tile([P, HEADS], F32, name="neg_max%d" % b) for b in range(BLOCKS)]
-        neg_max_half = sb.tile([P, 1], F32, name="neg_max_half")
         sums = [sb.tile([P, HEADS], F32, name="sums%d" % b) for b in range(BLOCKS)]
         spent = {
             (h, b): sb.tile([P, S], BF16, name="spent%d%d" % (h, b)) for h in range(HEADS) for b in range(BLOCKS)
@@ -87,7 +76,7 @@ def tile_picked_ymedu_mean_p_kernel(
         spent[2, 0] = reused.tile([P, S], BF16, name="spent_held", offset=26 * KIB - KIB // 2)
         late = sb.tile([P, 2], F32, name="late")
         total_offset = {(0, 0): 28 * KIB, (2, 0): 26 * KIB}
-        score_offset = {(0, 0): 4 * KIB, (0, 1): 22 * KIB, (1, 0): 8 * KIB, (2, 1): 24 * KIB}
+        score_offset = {(0, 0): 4 * KIB, (0, 1): 6 * KIB, (1, 0): 8 * KIB, (1, 1): 10 * KIB, (2, 1): 24 * KIB}
 
         def cast(dst, src, engine_copy):
             engine_copy(dst.rearrange("p (c n) j -> p c j n", n=4), src.rearrange("p j (c n) -> p c j n", n=4))
@@ -103,21 +92,17 @@ def tile_picked_ymedu_mean_p_kernel(
                 h_codes[h, first + b] = codes[:, b * P : (b + 1) * P]
                 h_bytes[h, first + b] = plane[:, b * P : (b + 1) * P]
 
-        def multiply(h, b, c, bank):
+        def multiply_unit(h, b):
+            banks[h, b, 0] = psum.tile([P, S], F32, name="bank%d%d" % (h, b))
             nc.tensor.matmul_mx(
-                out=bank,
+                out=banks[h, b, 0][:],
                 lhsT=h_codes[h, b].bitcast(FP8X4),
                 lhsT_scale=h_bytes[h, b],
-                rhs=x_codes[:, c * HALF : (c + 1) * HALF].bitcast(FP8X4),
-                rhs_scale=x_bytes[c][:],
+                rhs=x_codes[:].bitcast(FP8X4),
+                rhs_scale=x_bytes[:],
                 start=True,
                 stop=True,
             )
-
-        def multiply_unit(h, b):
-            banks[h, b, 0] = psum.tile([P, S], F32, name="bank%d%d" % (h, b))
-            for c in range(2):
-                multiply(h, b, c, banks[h, b, 0][:, c * HALF : (c + 1) * HALF])
 
         def scores(h, b):
             if (h, b) in score_offset:
@@ -160,40 +145,27 @@ def tile_picked_ymedu_mean_p_kernel(
             nc.scalar.activation(mean[:], neg_total[HEADS - 1, b][:], ACT.Exp, bias=shift[b][:], scale=-1.0 / HEADS)
             return mean
 
-        halves = [picks[:, c * HALF // 16 : (c + 1) * HALF // 16] for c in range(2)]
         nc.vector.tensor_copy(x_codes[:], table_words[:].indirect(picks[:]))
-        nc.vector.tensor_copy(x_bytes[0][:], table_scales[:].indirect(halves[0]))
-        for b in range(BLOCKS):
-            grouped[0, b] = sb.tile([P, P, PACK], BF16, name="grouped0%d" % b, align_bytes=64)
-            cast(grouped[0, b][:], raw[0, b], nc.scalar.copy)
-        quantise(0, 0, grouped[0, 0])
-        nc.vector.tensor_copy(x_bytes[1][:], table_scales[:].indirect(halves[1]))
-        for c in range(2):
-            banks[0, 0, c * HALF] = psum.tile([P, HALF], F32, name="bank00%d" % c)
-            multiply(0, 0, c, banks[0, 0, c * HALF][:])
-        quantise(0, 1, grouped[0, 1])
-        multiply_unit(0, 1)
-        grouped[1] = reused.tile([P, V, PACK], BF16, name="grouped1", offset=22 * KIB, align_bytes=64)
-        cast(grouped[1][:, 0:P, :], raw[1, 0], nc.scalar.copy)
-        cast(grouped[1][:, P:V, :], raw[1, 1], nc.vector.tensor_copy)
-        first = scores(0, 0)
-        nc.vector.tensor_scalar(
-            first[:, 0:HALF], banks[0, 0, 0][:], -1.0, None, ALU.mult, ALU.min, accum_out=neg_max_half[:]
-        )
-        quantise(1, 0, grouped[1])
-        for b in range(BLOCKS):
-            multiply_unit(1, b)
-        nc.vector.tensor_scalar(
-            first[:, HALF:S], banks[0, 0, HALF][:], -1.0, neg_max_half[:], ALU.mult, ALU.min,
-            accum_out=neg_max[0][:, 0:1],
-        )
-        leave_psum(0, 1)
-        for b in range(BLOCKS):
-            grouped[2, b] = sb.tile([P, P, PACK], BF16, name="grouped2%d" % b, align_bytes=64)
-            cast(grouped[2, b][:], raw[2, b], nc.scalar.copy)
-        for b in range(BLOCKS):
-            quantise(2, b, grouped[2, b])
-            multiply_unit(2, b)
+        nc.vector.tensor_copy(x_bytes[:], table_scales[:].indirect(picks[:]))
+        for h in range(HEADS):
+            for b in range(BLOCKS):
+                if b == 1 and h < 2:
+                    grouped[h, b] = reused.tile(
+                        [P, P, PACK], BF16, name="grouped%d%d" % (h, b), offset=22 * KIB, align_bytes=64
+                    )
+                else:
+                    grouped[h, b] = sb.tile([P, P, PACK], BF16, name="grouped%d%d" % (h, b), align_bytes=64)
+                cast(grouped[h, b][:], raw[h, b], nc.vector.tensor_copy if (h, b) == (1, 1) else nc.scalar.copy)
+                if h == 0:
+                    quantise(h, b, grouped[h, b])
+                    multiply_unit(h, b)
+            if h > 0:
+                for b in range(BLOCKS):
+                    quantise(h, b, grouped[h, b])
+                    multiply_unit(h, b)
+            if h == 1:
+                leave_psum(0, 0)
+                leave_psum(0, 1)
         leave_psum(1, 0)
         row_sums(0, 0)
         leave_psum(1, 1)
@@ -217,10 +189,19 @@ def tile_picked_ymedu_mean_p_kernel(
         shift.append(row_shift(1))
         nc.gpsimd.tensor_tensor(root[1][:], late[:], minus_third[:], ALU.pow)
         fetch(2, 0)
-        fetch(2, 1)
+        last = sb.tile([P, U], F32, name="neg_total21")
+        spans = [slice(c, c + U // 2) for c in range(0, U, U // 2)]
+        for span in spans:
+            window = neg_scores[2, 1][:].indirect(paths[2][:, span.start // 16 : span.stop // 16])
+            nc.vector.tensor_tensor(last[:, span], window, neg_total[1, 1][:, span], ALU.add)
         result = [sb.tile([P, U], F32, name="result%d" % b) for b in range(BLOCKS)]
-        means = [exp_mean(b) for b in range(BLOCKS)]
-        nc.scalar.activation(result[0][:], means[0][:], ACT.Identity, scale=root[0][:])
+        mean = [exp_mean(0), sb.tile([P, U], F32, name="mean1")]
+        for span in spans:
+            nc.scalar.activation(mean[1][:, span], last[:, span], ACT.Exp, bias=shift[1][:], scale=-1.0 / HEADS)
+        nc.scalar.activation(result[0][:], mean[0][:], ACT.Identity, scale=root[0][:])
         nc.sync.dma_start(out=out[0:P, :], in_=result[0][:])
-        nc.vector.tensor_scalar(result[1][:], means[1][:], root[1][:, 0:1], root[1][:, 1:2], ALU.mult, ALU.mult)
-        nc.sync.dma_start(out=out[P:V, :], in_=result[1][:])
+        for span in spans:
+            nc.vector.tensor_scalar(
+                result[1][:, span], mean[1][:, span], root[1][:, 0:1], root[1][:, 1:2], ALU.mult, ALU.mult
+            )
+            nc.sync.dma_start(out=out[P:V, span], in_=result[1][:, span])

@@ -149,13 +149,21 @@ def tile_picked_ymedu_mean_p_kernel(
         nc.vector.tensor_copy(x_bytes[:], table_scales[:].indirect(picks[:]))
         for h in range(HEADS):
             for b in range(BLOCKS):
-                if b == 1 and h < 2:
+                if b == 1:
                     grouped[h, b] = reused.tile(
                         [P, P, PACK], BF16, name="grouped%d%d" % (h, b), offset=22 * KIB, align_bytes=64
                     )
                 else:
                     grouped[h, b] = sb.tile([P, P, PACK], BF16, name="grouped%d%d" % (h, b), align_bytes=64)
-                cast(grouped[h, b][:], raw[h, b], nc.vector.tensor_copy if (h, b) == (1, 1) else nc.scalar.copy)
+                if (h, b) == (2, 1):
+                    cast(grouped[h, b][:, 0 : P // 2, :], raw[h, b][:, :, 0 : P // 2], nc.scalar.copy)
+                    nc.gpsimd.tensor_scalar(
+                        grouped[h, b][:, P // 2 : P, :],
+                        raw[h, b][:, :, P // 2 : P].rearrange("p j w -> p w j"),
+                        1.0, 0.0, ALU.mult, ALU.add,
+                    )
+                else:
+                    cast(grouped[h, b][:], raw[h, b], nc.vector.tensor_copy if (h, b) == (1, 1) else nc.scalar.copy)
                 if h == 0:
                     quantise(h, b, grouped[h, b])
                     multiply_unit(h, b)

@@ -1,3 +1,4 @@
+import math
 from contextlib import ExitStack
 
 import concourse.mybir as mybir
@@ -14,13 +15,27 @@ U8 = mybir.dt.uint8
 FP8X4 = mybir.dt.float8_e4m3fn_x4
 ALU = mybir.AluOpType
 ACT = mybir.ActivationFunctionType
+AXIS = mybir.AxisListType
 
 P = 128
 PACK = 4
 HEADS = 3
 BLOCKS = V // P
-HALF = S // 2
 KIB = 1024
+
+LN2 = math.log(2.0)
+BIT_STEP = LN2 / 2**23
+MANTISSA_GAP = math.log(1.0 / LN2) / LN2 - (1.0 / LN2 - 1.0)
+BIT_ZERO = LN2 * (127.0 - MANTISSA_GAP / 2)
+DEGREE = 11
+SERIES = [
+    (-1) ** i * sum(math.factorial(k) / (math.factorial(i) * math.factorial(k - i)) / k for k in range(max(i, 1), DEGREE + 1))
+    for i in range(DEGREE + 1)
+]
+GUESS_STEP = 2 * DEGREE + 1
+MAX_STEP = GUESS_STEP + 1
+LAST_STEP = MAX_STEP + HEADS
+STEPS = LAST_STEP + 1
 
 
 def tile_picked_ymedu_mean_p_kernel(
@@ -58,92 +73,81 @@ def tile_picked_ymedu_mean_p_kernel(
             paths.append(lists.tile([P, U // 16], U16, name="path%d" % h))
             nc.sync.dma_start(paths[h][:], tree)
 
-        minus_one = sb.tile([P, 2], F32, name="minus_one")
-        nc.vector.memset(minus_one[:], -1.0)
-        minus_third = sb.tile([P, 2], F32, name="minus_third")
-        nc.scalar.activation(minus_third[:], minus_one[:], ACT.Identity, scale=1.0 / HEADS)
+        factors = sb.tile([P, BLOCKS * STEPS], F32, name="factors")
+        terms = sb.tile([P, BLOCKS * STEPS], F32, name="terms")
+        ones = sb.tile([P, BLOCKS], F32, name="ones")
+        nc.vector.memset(ones[:], 1.0)
+        nc.vector.memset(factors[:], 1.0)
+        nc.vector.memset(terms[:], 0.0)
+        nc.vector.memset(factors[:, 0::STEPS], 0.0)
+        nc.scalar.activation(factors[:, LAST_STEP::STEPS], ones[:], ACT.Identity, scale=1.0 / HEADS)
+        for i in range(DEGREE + 1):
+            nc.vector.tensor_scalar(terms[:, 2 * (DEGREE - i) :: STEPS], ones[:], SERIES[i], None, ALU.mult)
 
         x_codes = sb.tile([P, S], U32, name="x_codes", align_bytes=64)
         x_bytes = sb.tile([P, S], U8, name="x_bytes", align_bytes=64)
         grouped, h_codes, h_bytes, banks = {}, {}, {}, {}
         neg_scores, neg_total = {}, {}
-        neg_max = [sb.tile([P, HEADS], F32, name="neg_max%d" % b) for b in range(BLOCKS)]
-        sums = [sb.tile([P, HEADS], F32, name="sums%d" % b) for b in range(BLOCKS)]
-        spent = {
-            (h, b): sb.tile([P, S], BF16, name="spent%d%d" % (h, b)) for h in range(HEADS) for b in range(BLOCKS)
-        }
-        spent[1, 1] = reused.tile([P, S], BF16, name="spent_late", offset=28 * KIB)
-        spent[2, 0] = reused.tile([P, S], BF16, name="spent_held", offset=26 * KIB - KIB // 2)
-        late = sb.tile([P, 2], F32, name="late")
-        total_offset = {(0, 0): 28 * KIB, (2, 0): 26 * KIB}
-        score_offset = {(0, 0): 4 * KIB, (0, 1): 6 * KIB, (1, 0): 8 * KIB, (1, 1): 10 * KIB, (2, 1): 24 * KIB}
+        sums = sb.tile([P, BLOCKS * HEADS], F32, name="sums")
+        score_offset = {(0, 0): 4 * KIB, (0, 1): 6 * KIB, (1, 0): 8 * KIB, (1, 1): 10 * KIB}
+        spent_offset = {(2, 1): 24 * KIB}
+        total_offset = {(0, 0, 0): 28 * KIB, (0, 1, U // 2): 28 * KIB, (2, 1, 0): 24 * KIB, (2, 1, U // 2): 26 * KIB}
+
+        def placed(name, key, shape, dtype, offsets):
+            label = name + "_".join("%d" % n for n in key)
+            if key in offsets:
+                return reused.tile(shape, dtype, name=label, offset=offsets[key])
+            return sb.tile(shape, dtype, name=label)
+
+        def neg_max(h, b):
+            column = b * STEPS + MAX_STEP + h
+            return terms[:, column : column + 1]
 
         def cast(dst, src, engine_copy):
             engine_copy(dst.rearrange("p (c n) j -> p c j n", n=4), src.rearrange("p j (c n) -> p c j n", n=4))
 
-        def quantise(h, first, source):
-            width = source.shape[1]
-            codes = sb.tile([P, width], U32, name="h_codes%d%d" % (h, first), align_bytes=64)
-            plane = sb.tile([P, width], U8, name="h_bytes%d%d" % (h, first), align_bytes=64)
+        def quantise(h, b):
+            codes = sb.tile([P, P], U32, name="h_codes%d%d" % (h, b), align_bytes=64)
+            plane = sb.tile([P, P], U8, name="h_bytes%d%d" % (h, b), align_bytes=64)
             nc.vector.quantize_mx(
-                out=codes[:].bitcast(FP8X4), scales=plane[:], in_=source[:].rearrange("p w j -> p (w j)")
+                out=codes[:].bitcast(FP8X4), scales=plane[:], in_=grouped[h, b][:].rearrange("p w j -> p (w j)")
             )
-            for b in range(width // P):
-                h_codes[h, first + b] = codes[:, b * P : (b + 1) * P]
-                h_bytes[h, first + b] = plane[:, b * P : (b + 1) * P]
+            h_codes[h, b], h_bytes[h, b] = codes, plane
 
         def multiply_unit(h, b):
-            banks[h, b, 0] = psum.tile([P, S], F32, name="bank%d%d" % (h, b))
+            banks[h, b] = psum.tile([P, S], F32, name="bank%d%d" % (h, b))
             nc.tensor.matmul_mx(
-                out=banks[h, b, 0][:],
-                lhsT=h_codes[h, b].bitcast(FP8X4),
-                lhsT_scale=h_bytes[h, b],
+                out=banks[h, b][:],
+                lhsT=h_codes[h, b][:].bitcast(FP8X4),
+                lhsT_scale=h_bytes[h, b][:],
                 rhs=x_codes[:].bitcast(FP8X4),
                 rhs_scale=x_bytes[:],
                 start=True,
                 stop=True,
             )
 
-        def scores(h, b):
-            if (h, b) in score_offset:
-                neg_scores[h, b] = reused.tile([P, S], F32, name="neg_scores%d%d" % (h, b), offset=score_offset[h, b])
-            else:
-                neg_scores[h, b] = sb.tile([P, S], F32, name="neg_scores%d%d" % (h, b))
-            return neg_scores[h, b]
-
         def leave_psum(h, b):
+            neg_scores[h, b] = placed("neg_scores", (h, b), [P, S], F32, score_offset)
             nc.vector.tensor_scalar(
-                scores(h, b)[:], banks[h, b, 0][:], -1.0, None, ALU.mult, ALU.min, accum_out=neg_max[b][:, h : h + 1]
+                neg_scores[h, b][:], banks[h, b][:], -1.0, None, ALU.mult, ALU.min, accum_out=neg_max(h, b)
             )
 
         def row_sums(h, b):
-            unused = spent[h, b][:]
+            unused = placed("spent", (h, b), [P, S], BF16, spent_offset)
+            column = b * HEADS + h
             nc.scalar.activation(
-                unused, neg_scores[h, b][:], ACT.Exp, bias=neg_max[b][:, h : h + 1], scale=-1.0,
-                accum_out=late[:, 1:2] if (h, b) == (2, 1) else sums[b][:, h : h + 1],
+                unused[:], neg_scores[h, b][:], ACT.Exp, bias=neg_max(h, b), scale=-1.0,
+                accum_out=sums[:, column : column + 1],
             )
 
-        def fetch(h, b):
-            window = neg_scores[h, b][:].indirect(paths[h][:])
-            if (h, b) in total_offset:
-                neg_total[h, b] = reused.tile([P, U], F32, name="neg_total%d%d" % (h, b), offset=total_offset[h, b])
-            else:
-                neg_total[h, b] = sb.tile([P, U], F32, name="neg_total%d%d" % (h, b))
+        def fetch(h, b, span):
+            key = (h, b, span.start)
+            neg_total[key] = placed("neg_total", key, [P, span.stop - span.start], F32, total_offset)
+            window = neg_scores[h, b][:].indirect(paths[h][:, span.start // 16 : span.stop // 16])
             if h == 0:
-                nc.scalar.activation(neg_total[h, b][:], window, ACT.Copy)
+                nc.scalar.activation(neg_total[key][:], window, ACT.Copy)
             else:
-                nc.vector.tensor_tensor(neg_total[h, b][:], window, neg_total[h - 1, b][:], ALU.add)
-
-        def row_shift(b):
-            thirds = sb.tile([P, HEADS], F32, name="thirds%d" % b)
-            total = sb.tile([P, 1], F32, name="shift%d" % b)
-            nc.scalar.activation(thirds[:], neg_max[b][:], ACT.Identity, scale=1.0 / HEADS, accum_out=total[:])
-            return total
-
-        def exp_mean(b):
-            mean = sb.tile([P, U], F32, name="mean%d" % b)
-            nc.scalar.activation(mean[:], neg_total[HEADS - 1, b][:], ACT.Exp, bias=shift[b][:], scale=-1.0 / HEADS)
-            return mean
+                nc.vector.tensor_tensor(neg_total[key][:], window, neg_total[h - 1, b, span.start][:], ALU.add)
 
         nc.vector.tensor_copy(x_codes[:], table_words[:].indirect(picks[:]))
         nc.vector.tensor_copy(x_bytes[:], table_scales[:].indirect(picks[:]))
@@ -156,60 +160,59 @@ def tile_picked_ymedu_mean_p_kernel(
                 else:
                     grouped[h, b] = sb.tile([P, P, PACK], BF16, name="grouped%d%d" % (h, b), align_bytes=64)
                 if (h, b) == (2, 1):
-                    cast(grouped[h, b][:, 0 : P // 2, :], raw[h, b][:, :, 0 : P // 2], nc.scalar.copy)
                     nc.gpsimd.tensor_scalar(
-                        grouped[h, b][:, P // 2 : P, :],
-                        raw[h, b][:, :, P // 2 : P].rearrange("p j w -> p w j"),
-                        1.0, 0.0, ALU.mult, ALU.add,
+                        grouped[h, b][:], raw[h, b].rearrange("p j w -> p w j"), 1.0, 0.0, ALU.mult, ALU.add
                     )
                 else:
                     cast(grouped[h, b][:], raw[h, b], nc.vector.tensor_copy if (h, b) == (1, 1) else nc.scalar.copy)
                 if h == 0:
-                    quantise(h, b, grouped[h, b])
+                    quantise(h, b)
                     multiply_unit(h, b)
             if h > 0:
                 for b in range(BLOCKS):
-                    quantise(h, b, grouped[h, b])
+                    quantise(h, b)
                     multiply_unit(h, b)
             if h == 1:
                 leave_psum(0, 0)
                 leave_psum(0, 1)
-        leave_psum(1, 0)
-        row_sums(0, 0)
-        leave_psum(1, 1)
-        leave_psum(2, 0)
-        fetch(0, 0)
-        row_sums(1, 0)
-        fetch(0, 1)
-        row_sums(2, 0)
-        fetch(1, 0)
-        fetch(1, 1)
-        norm = sb.tile([P, 1], F32, name="norm")
-        root = [sb.tile([P, 1 + b], F32, name="root%d" % b) for b in range(BLOCKS)]
-        nc.vector.tensor_scalar(norm[:], sums[0][:, 0:1], sums[0][:, 1:2], sums[0][:, 2:3], ALU.mult, ALU.mult)
-        nc.gpsimd.tensor_tensor(root[0][:], norm[:], minus_third[:, 0:1], ALU.pow)
-        leave_psum(2, 1)
-        row_sums(0, 1)
-        row_sums(1, 1)
-        shift = [row_shift(0)]
-        nc.scalar.activation(late[:, 0:1], sums[1][:, 0:1], ACT.Identity, scale=sums[1][:, 1:2])
-        row_sums(2, 1)
-        shift.append(row_shift(1))
-        nc.gpsimd.tensor_tensor(root[1][:], late[:], minus_third[:], ALU.pow)
-        fetch(2, 0)
-        last = sb.tile([P, U], F32, name="neg_total21")
-        spans = [slice(c, c + U // 2) for c in range(0, U, U // 2)]
-        for span in spans:
-            window = neg_scores[2, 1][:].indirect(paths[2][:, span.start // 16 : span.stop // 16])
-            nc.vector.tensor_tensor(last[:, span], window, neg_total[1, 1][:, span], ALU.add)
-        result = [sb.tile([P, U], F32, name="result%d" % b) for b in range(BLOCKS)]
-        mean = [exp_mean(0), sb.tile([P, U], F32, name="mean1")]
-        for span in spans:
-            nc.scalar.activation(mean[1][:, span], last[:, span], ACT.Exp, bias=shift[1][:], scale=-1.0 / HEADS)
-        nc.scalar.activation(result[0][:], mean[0][:], ACT.Identity, scale=root[0][:])
-        nc.sync.dma_start(out=out[0:P, :], in_=result[0][:])
-        for span in spans:
-            nc.vector.tensor_scalar(
-                result[1][:, span], mean[1][:, span], root[1][:, 0:1], root[1][:, 1:2], ALU.mult, ALU.mult
-            )
-            nc.sync.dma_start(out=out[P:V, span], in_=result[1][:, span])
+        for h in (1, 2):
+            for b in range(BLOCKS):
+                leave_psum(h, b)
+        whole = slice(0, U)
+        halves = [slice(c, c + U // 2) for c in range(0, U, U // 2)]
+        for h in range(HEADS):
+            for b in range(BLOCKS):
+                row_sums(h, b)
+            if h == 0:
+                fetch(0, 0, whole)
+            if h == 1:
+                fetch(0, 1, halves[0])
+        fetch(1, 0, whole)
+        fetch(0, 1, halves[1])
+        fetch(1, 1, halves[0])
+        fetch(2, 0, whole)
+
+        product = reused.tile([P, BLOCKS], F32, name="product", offset=26 * KIB)
+        nc.vector.tensor_reduce(product[:], sums[:].rearrange("p (b h) -> p b h", h=HEADS), AXIS.X, ALU.mult)
+        pairs = factors[:].rearrange("p (b s) -> p b s", s=STEPS)[:, :, 1:GUESS_STEP]
+        copies = [P, BLOCKS, DEGREE]
+        bits = product[:].bitcast(U32)
+        nc.scalar.activation(
+            pairs[:, :, 1::2], bits.unsqueeze(2).to_broadcast(copies), ACT.Exp, bias=BIT_ZERO, scale=-BIT_STEP
+        )
+        nc.scalar.activation(pairs[:, :, 0::2], product[:].unsqueeze(2).to_broadcast(copies), ACT.Copy)
+        nc.scalar.activation(terms[:, GUESS_STEP::STEPS], bits, ACT.Identity, bias=BIT_ZERO, scale=-BIT_STEP)
+        fetch(2, 1, halves[0])
+        fetch(1, 1, halves[1])
+        running = sb.tile([P, BLOCKS * STEPS], F32, name="running")
+        nc.vector.tensor_tensor_scan(running[:], factors[:], terms[:], 0.0, ALU.mult, ALU.add)
+        fetch(2, 1, halves[1])
+        for b, spans in enumerate(([whole], halves)):
+            result = sb.tile([P, U], F32, name="result%d" % b)
+            column = b * STEPS + LAST_STEP
+            for span in spans:
+                nc.scalar.activation(
+                    result[:, span], neg_total[HEADS - 1, b, span.start][:], ACT.Exp,
+                    bias=running[:, column : column + 1], scale=-1.0 / HEADS,
+                )
+                nc.sync.dma_start(out=out[b * P : (b + 1) * P, span], in_=result[:, span])

@@ -22,6 +22,7 @@ PACK = 4
 HEADS = 3
 BLOCKS = V // P
 KIB = 1024
+FIRST_WORDS = T // 2
 
 LN2 = math.log(2.0)
 BIT_STEP = LN2 / 2**23
@@ -55,17 +56,17 @@ def tile_picked_ymedu_mean_p_kernel(
         table_scales = sb.tile([P, T], U8, name="table_scales", align_bytes=64)
         nc.vector.memset(table_scales[:].bitcast(I32), 0)
         table_words = sb.tile([P, T], U32, name="table_words", align_bytes=64)
-        nc.sync.dma_start(
-            out=table_words[:].bitcast(I32),
-            in_=x_words[0].rearrange("p n t -> p (n t)").bitcast(I32),
-        )
+        words = x_words[0].rearrange("p n t -> p (n t)").bitcast(I32)
+        nc.sync.dma_start(out=table_words[:, 0:FIRST_WORDS].bitcast(I32), in_=words[:, 0:FIRST_WORDS])
         picks = lists.tile([P, S // 16], U16, name="picks")
         nc.sync.dma_start(picks[:], offs)
         for q in range(4):
-            nc.sync.dma_start(
+            queue = nc.sync if q < 2 else nc.scalar
+            queue.dma_start(
                 out=table_scales[32 * q : 32 * q + 4, :].bitcast(I32),
                 in_=x_scales[0, 4 * q : 4 * q + 4, :].bitcast(I32),
             )
+        nc.sync.dma_start(out=table_words[:, FIRST_WORDS:T].bitcast(I32), in_=words[:, FIRST_WORDS:T])
         for h in range(HEADS):
             nc.sync.dma_start(out=raws[h][:], in_=states[h])
         paths = []
@@ -149,11 +150,11 @@ def tile_picked_ymedu_mean_p_kernel(
             else:
                 nc.vector.tensor_tensor(neg_total[key][:], window, neg_total[h - 1, b, span.start][:], ALU.add)
 
-        nc.vector.tensor_copy(x_codes[:], table_words[:].indirect(picks[:]))
         nc.vector.tensor_copy(x_bytes[:], table_scales[:].indirect(picks[:]))
+        nc.vector.tensor_copy(x_codes[:], table_words[:].indirect(picks[:]))
         for h in range(HEADS):
             for b in range(BLOCKS):
-                if b == 1:
+                if b == 1 and h > 0:
                     grouped[h, b] = reused.tile(
                         [P, P, PACK], BF16, name="grouped%d%d" % (h, b), offset=22 * KIB, align_bytes=64
                     )

@@ -22,7 +22,7 @@ PACK = 4
 HEADS = 3
 BLOCKS = V // P
 KIB = 1024
-FIRST_WORDS = T // 2
+FIRST_WORDS = 5 * T // 8
 
 LN2 = math.log(2.0)
 BIT_STEP = LN2 / 2**23
@@ -61,7 +61,7 @@ def tile_picked_ymedu_mean_p_kernel(
         picks = lists.tile([P, S // 16], U16, name="picks")
         nc.sync.dma_start(picks[:], offs)
         for q in range(4):
-            queue = nc.sync if q < 2 else nc.scalar
+            queue = nc.sync if q < 3 else nc.scalar
             queue.dma_start(
                 out=table_scales[32 * q : 32 * q + 4, :].bitcast(I32),
                 in_=x_scales[0, 4 * q : 4 * q + 4, :].bitcast(I32),
@@ -107,20 +107,23 @@ def tile_picked_ymedu_mean_p_kernel(
         def cast(dst, src, engine_copy):
             engine_copy(dst.rearrange("p (c n) j -> p c j n", n=4), src.rearrange("p j (c n) -> p c j n", n=4))
 
-        def quantise(h, b):
-            codes = sb.tile([P, P], U32, name="h_codes%d%d" % (h, b), align_bytes=64)
-            plane = sb.tile([P, P], U8, name="h_bytes%d%d" % (h, b), align_bytes=64)
+        def quantise(h, first, source):
+            width = source.shape[1]
+            codes = sb.tile([P, width], U32, name="h_codes%d%d" % (h, first), align_bytes=64)
+            plane = sb.tile([P, width], U8, name="h_bytes%d%d" % (h, first), align_bytes=64)
             nc.vector.quantize_mx(
-                out=codes[:].bitcast(FP8X4), scales=plane[:], in_=grouped[h, b][:].rearrange("p w j -> p (w j)")
+                out=codes[:].bitcast(FP8X4), scales=plane[:], in_=source[:].rearrange("p w j -> p (w j)")
             )
-            h_codes[h, b], h_bytes[h, b] = codes, plane
+            for b in range(width // P):
+                h_codes[h, first + b] = codes[:, b * P : (b + 1) * P]
+                h_bytes[h, first + b] = plane[:, b * P : (b + 1) * P]
 
         def multiply_unit(h, b):
             banks[h, b] = psum.tile([P, S], F32, name="bank%d%d" % (h, b))
             nc.tensor.matmul_mx(
                 out=banks[h, b][:],
-                lhsT=h_codes[h, b][:].bitcast(FP8X4),
-                lhsT_scale=h_bytes[h, b][:],
+                lhsT=h_codes[h, b].bitcast(FP8X4),
+                lhsT_scale=h_bytes[h, b],
                 rhs=x_codes[:].bitcast(FP8X4),
                 rhs_scale=x_bytes[:],
                 start=True,
@@ -152,30 +155,29 @@ def tile_picked_ymedu_mean_p_kernel(
 
         nc.vector.tensor_copy(x_bytes[:], table_scales[:].indirect(picks[:]))
         nc.vector.tensor_copy(x_codes[:], table_words[:].indirect(picks[:]))
-        for h in range(HEADS):
+        for h in (0, 1):
             for b in range(BLOCKS):
-                if b == 1 and h > 0:
+                if h == 1:
                     grouped[h, b] = reused.tile(
-                        [P, P, PACK], BF16, name="grouped%d%d" % (h, b), offset=22 * KIB, align_bytes=64
+                        [P, P, PACK], BF16, name="grouped%d%d" % (h, b), offset=(20 + b) * KIB, align_bytes=64
                     )
                 else:
                     grouped[h, b] = sb.tile([P, P, PACK], BF16, name="grouped%d%d" % (h, b), align_bytes=64)
-                if (h, b) == (2, 1):
-                    nc.gpsimd.tensor_scalar(
-                        grouped[h, b][:], raw[h, b].rearrange("p j w -> p w j"), 1.0, 0.0, ALU.mult, ALU.add
-                    )
-                else:
-                    cast(grouped[h, b][:], raw[h, b], nc.vector.tensor_copy if (h, b) == (1, 1) else nc.scalar.copy)
+                cast(grouped[h, b][:], raw[h, b], nc.vector.tensor_copy if (h, b) == (1, 1) else nc.scalar.copy)
                 if h == 0:
-                    quantise(h, b)
+                    quantise(h, b, grouped[h, b])
                     multiply_unit(h, b)
-            if h > 0:
-                for b in range(BLOCKS):
-                    quantise(h, b)
-                    multiply_unit(h, b)
-            if h == 1:
-                leave_psum(0, 0)
-                leave_psum(0, 1)
+        for b in range(BLOCKS):
+            quantise(1, b, grouped[1, b])
+            multiply_unit(1, b)
+        for b in range(BLOCKS):
+            leave_psum(0, b)
+        last = reused.tile([P, V, PACK], BF16, name="grouped2", offset=20 * KIB, align_bytes=64)
+        cast(last[:, 0:P, :], raw[2, 0], nc.scalar.copy)
+        nc.gpsimd.tensor_scalar(last[:, P:V, :], raw[2, 1].rearrange("p j w -> p w j"), 1.0, 0.0, ALU.mult, ALU.add)
+        quantise(2, 0, last)
+        for b in range(BLOCKS):
+            multiply_unit(2, b)
         for h in (1, 2):
             for b in range(BLOCKS):
                 leave_psum(h, b)

@@ -210,12 +210,11 @@ def tile_picked_ymedu_mean_p_kernel(
         running = sb.tile([P, BLOCKS * STEPS], F32, name="running")
         nc.vector.tensor_tensor_scan(running[:], factors[:], terms[:], 0.0, ALU.mult, ALU.add)
         fetch(2, 1, halves[1])
-        for b, spans in enumerate(([whole], halves)):
-            result = sb.tile([P, U], F32, name="result%d" % b)
+        for b, span in ((1, halves[0]), (0, whole), (1, halves[1])):
+            result = sb.tile([P, span.stop - span.start], F32, name="result%d_%d" % (b, span.start))
             column = b * STEPS + LAST_STEP
-            for span in spans:
-                nc.scalar.activation(
-                    result[:, span], neg_total[HEADS - 1, b, span.start][:], ACT.Exp,
-                    bias=running[:, column : column + 1], scale=-1.0 / HEADS,
-                )
-                nc.sync.dma_start(out=out[b * P : (b + 1) * P, span], in_=result[:, span])
+            nc.scalar.activation(
+                result[:], neg_total[HEADS - 1, b, span.start][:], ACT.Exp,
+                bias=running[:, column : column + 1], scale=-1.0 / HEADS,
+            )
+            nc.sync.dma_start(out=out[b * P : (b + 1) * P, span], in_=result[:])

@@ -167,7 +167,7 @@ def tile_picked_ymedu_mean_p_kernel(
                 if h == 0:
                     quantise(h, b, grouped[h, b])
                     multiply_unit(h, b)
-        for b in range(BLOCKS):
+        for b in (1, 0):
             quantise(1, b, grouped[1, b])
             multiply_unit(1, b)
         for b in range(BLOCKS):
@@ -178,13 +178,12 @@ def tile_picked_ymedu_mean_p_kernel(
         quantise(2, 0, last)
         for b in range(BLOCKS):
             multiply_unit(2, b)
-        for h in (1, 2):
-            for b in range(BLOCKS):
-                leave_psum(h, b)
+        for h, b in ((1, 1), (1, 0), (2, 0), (2, 1)):
+            leave_psum(h, b)
         whole = slice(0, U)
         halves = [slice(c, c + U // 2) for c in range(0, U, U // 2)]
         for h in range(HEADS):
-            for b in range(BLOCKS):
+            for b in (1, 0) if h == 1 else (0, 1):
                 row_sums(h, b)
             if h == 0:
                 fetch(0, 0, whole)

@@ -83,7 +83,7 @@ def tile_picked_ymedu_mean_p_kernel(
         nc.vector.memset(factors[:, 0::STEPS], 0.0)
         nc.scalar.activation(factors[:, LAST_STEP::STEPS], ones[:], ACT.Identity, scale=1.0 / HEADS)
         for i in range(DEGREE + 1):
-            nc.vector.tensor_scalar(terms[:, 2 * (DEGREE - i) :: STEPS], ones[:], SERIES[i], None, ALU.mult)
+            nc.scalar.activation(terms[:, 2 * (DEGREE - i) :: STEPS], ones[:], ACT.Identity, scale=SERIES[i])
 
         x_codes = sb.tile([P, S], U32, name="x_codes", align_bytes=64)
         x_bytes = sb.tile([P, S], U8, name="x_bytes", align_bytes=64)

@@ -76,14 +76,13 @@ def tile_picked_ymedu_mean_p_kernel(
 
         factors = sb.tile([P, BLOCKS * STEPS], F32, name="factors")
         terms = sb.tile([P, BLOCKS * STEPS], F32, name="terms")
-        ones = sb.tile([P, BLOCKS], F32, name="ones")
-        nc.vector.memset(ones[:], 1.0)
         nc.vector.memset(factors[:], 1.0)
         nc.vector.memset(terms[:], 0.0)
         nc.vector.memset(factors[:, 0::STEPS], 0.0)
-        nc.scalar.activation(factors[:, LAST_STEP::STEPS], ones[:], ACT.Identity, scale=1.0 / HEADS)
+        ones = factors[:, MAX_STEP::STEPS]
+        nc.scalar.activation(factors[:, LAST_STEP::STEPS], ones, ACT.Identity, scale=1.0 / HEADS)
         for i in range(DEGREE + 1):
-            nc.scalar.activation(terms[:, 2 * (DEGREE - i) :: STEPS], ones[:], ACT.Identity, scale=SERIES[i])
+            nc.scalar.activation(terms[:, 2 * (DEGREE - i) :: STEPS], ones, ACT.Identity, scale=SERIES[i])
 
         x_codes = sb.tile([P, S], U32, name="x_codes", align_bytes=64)
         x_bytes = sb.tile([P, S], U8, name="x_bytes", align_bytes=64)
@@ -91,7 +90,7 @@ def tile_picked_ymedu_mean_p_kernel(
         neg_scores, neg_total = {}, {}
         sums = sb.tile([P, BLOCKS * HEADS], F32, name="sums")
         score_offset = {(0, 0): 4 * KIB, (0, 1): 6 * KIB, (1, 0): 8 * KIB, (1, 1): 10 * KIB}
-        spent_offset = {(2, 1): 24 * KIB}
+        last_low = reused.tile([P, 1], F32, name="last_low", offset=24 * KIB)
         total_offset = {(0, 0, 0): 28 * KIB, (0, 1, U // 2): 28 * KIB, (2, 1, 0): 24 * KIB, (2, 1, U // 2): 26 * KIB}
 
         def placed(name, key, shape, dtype, offsets):
@@ -100,9 +99,12 @@ def tile_picked_ymedu_mean_p_kernel(
                 return reused.tile(shape, dtype, name=label, offset=offsets[key])
             return sb.tile(shape, dtype, name=label)
 
-        def neg_max(h, b):
+        def max_term(h, b):
             column = b * STEPS + MAX_STEP + h
             return terms[:, column : column + 1]
+
+        def neg_max(h, b):
+            return last_low[:] if (h, b) == (HEADS - 1, BLOCKS - 1) else max_term(h, b)
 
         def cast(dst, src, engine_copy):
             engine_copy(dst.rearrange("p (c n) j -> p c j n", n=4), src.rearrange("p j (c n) -> p c j n", n=4))
@@ -137,7 +139,7 @@ def tile_picked_ymedu_mean_p_kernel(
             )
 
         def row_sums(h, b):
-            unused = placed("spent", (h, b), [P, S], BF16, spent_offset)
+            unused = sb.tile([P, S], BF16, name="spent%d%d" % (h, b))
             column = b * HEADS + h
             nc.scalar.activation(
                 unused[:], neg_scores[h, b][:], ACT.Exp, bias=neg_max(h, b), scale=-1.0,
@@ -193,6 +195,7 @@ def tile_picked_ymedu_mean_p_kernel(
         fetch(0, 1, halves[1])
         fetch(1, 1, halves[0])
         fetch(2, 0, whole)
+        nc.vector.tensor_copy(max_term(HEADS - 1, BLOCKS - 1), last_low[:])
 
         product = reused.tile([P, BLOCKS], F32, name="product", offset=26 * KIB)
         nc.vector.tensor_reduce(product[:], sums[:].rearrange("p (b h) -> p b h", h=HEADS), AXIS.X, ALU.mult)

import math
from contextlib import ExitStack

import concourse.mybir as mybir

K, T, S, V, U = 512, 1024, 512, 256, 256
FLOPS = 3 * 2 * K * V * S

F32 = mybir.dt.float32
BF16 = mybir.dt.bfloat16
I32 = mybir.dt.int32
U32 = mybir.dt.uint32
U16 = mybir.dt.uint16
U8 = mybir.dt.uint8
FP8X4 = mybir.dt.float8_e4m3fn_x4
ALU = mybir.AluOpType
ACT = mybir.ActivationFunctionType
AXIS = mybir.AxisListType

P = 128
PACK = 4
HEADS = 3
BLOCKS = V // P
KIB = 1024
FIRST_WORDS = 5 * T // 8

LN2 = math.log(2.0)
BIT_STEP = LN2 / 2**23
MANTISSA_GAP = math.log(1.0 / LN2) / LN2 - (1.0 / LN2 - 1.0)
BIT_ZERO = LN2 * (127.0 - MANTISSA_GAP / 2)
DEGREE = 11
SERIES = [
    (-1) ** i * sum(math.factorial(k) / (math.factorial(i) * math.factorial(k - i)) / k for k in range(max(i, 1), DEGREE + 1))
    for i in range(DEGREE + 1)
]
GUESS_STEP = 2 * DEGREE + 1
MAX_STEP = GUESS_STEP + 1
LAST_STEP = MAX_STEP + HEADS
STEPS = LAST_STEP + 1


def tile_picked_ymedu_mean_p_kernel(
    tc, x_words, x_scales, h0, h1, h2, offs, tree1, tree2, tree3, out
):
    nc = tc.nc
    with ExitStack() as ctx:
        lists = ctx.enter_context(tc.tile_pool(name="lists", bufs=1))
        reused = ctx.enter_context(tc.tile_pool(name="reused", bufs=1))
        sb = ctx.enter_context(tc.tile_pool(name="sb", bufs=1))
        psum = ctx.enter_context(tc.psum_pool(name="psum", bufs=1))

        states = [h.rearrange("(p j) w -> p j w", j=PACK) for h in (h0, h1, h2)]
        raws = [reused.tile([P, PACK, V], F32, name="raw%d" % h, offset=4 * KIB * h) for h in range(HEADS)]
        raw = {(h, b): raws[h][:, :, b * P : (b + 1) * P] for h in range(HEADS) for b in range(BLOCKS)}

        table_scales = sb.tile([P, T], U8, name="table_scales", align_bytes=64)
        nc.vector.memset(table_scales[:].bitcast(I32), 0)
        table_words = sb.tile([P, T], U32, name="table_words", align_bytes=64)
        words = x_words[0].rearrange("p n t -> p (n t)").bitcast(I32)
        nc.sync.dma_start(out=table_words[:, 0:FIRST_WORDS].bitcast(I32), in_=words[:, 0:FIRST_WORDS])
        picks = lists.tile([P, S // 16], U16, name="picks")
        nc.sync.dma_start(picks[:], offs)
        for q in range(4):
            queue = nc.sync if q < 3 else nc.scalar
            queue.dma_start(
                out=table_scales[32 * q : 32 * q + 4, :].bitcast(I32),
                in_=x_scales[0, 4 * q : 4 * q + 4, :].bitcast(I32),
            )
        nc.sync.dma_start(out=table_words[:, FIRST_WORDS:T].bitcast(I32), in_=words[:, FIRST_WORDS:T])
        for h in range(HEADS):
            nc.sync.dma_start(out=raws[h][:], in_=states[h])
        paths = []
        for h, tree in enumerate((tree1, tree2, tree3)):
            paths.append(lists.tile([P, U // 16], U16, name="path%d" % h))
            nc.sync.dma_start(paths[h][:], tree)

        factors = sb.tile([P, BLOCKS * STEPS], F32, name="factors")
        terms = sb.tile([P, BLOCKS * STEPS], F32, name="terms")
        nc.vector.memset(factors[:], 1.0)
        nc.vector.memset(terms[:], 0.0)
        nc.vector.memset(factors[:, 0::STEPS], 0.0)
        ones = factors[:, MAX_STEP::STEPS]
        nc.scalar.activation(factors[:, LAST_STEP::STEPS], ones, ACT.Identity, scale=1.0 / HEADS)
        for i in range(DEGREE + 1):
            nc.scalar.activation(terms[:, 2 * (DEGREE - i) :: STEPS], ones, ACT.Identity, scale=SERIES[i])

        x_codes = sb.tile([P, S], U32, name="x_codes", align_bytes=64)
        x_bytes = sb.tile([P, S], U8, name="x_bytes", align_bytes=64)
        grouped, h_codes, h_bytes, banks = {}, {}, {}, {}
        neg_scores, neg_total = {}, {}
        sums = sb.tile([P, BLOCKS * HEADS], F32, name="sums")
        score_offset = {(0, 0): 4 * KIB, (0, 1): 6 * KIB, (1, 0): 8 * KIB, (1, 1): 10 * KIB}
        last_low = reused.tile([P, 1], F32, name="last_low", offset=24 * KIB)
        total_offset = {(0, 0, 0): 28 * KIB, (0, 1, U // 2): 28 * KIB, (2, 1, 0): 24 * KIB, (2, 1, U // 2): 26 * KIB}

        def placed(name, key, shape, dtype, offsets):
            label = name + "_".join("%d" % n for n in key)
            if key in offsets:
                return reused.tile(shape, dtype, name=label, offset=offsets[key])
            return sb.tile(shape, dtype, name=label)

        def max_term(h, b):
            column = b * STEPS + MAX_STEP + h
            return terms[:, column : column + 1]

        def neg_max(h, b):
            return last_low[:] if (h, b) == (HEADS - 1, BLOCKS - 1) else max_term(h, b)

        def cast(dst, src, engine_copy):
            engine_copy(dst.rearrange("p (c n) j -> p c j n", n=4), src.rearrange("p j (c n) -> p c j n", n=4))

        def quantise(h, first, source):
            width = source.shape[1]
            codes = sb.tile([P, width], U32, name="h_codes%d%d" % (h, first), align_bytes=64)
            plane = sb.tile([P, width], U8, name="h_bytes%d%d" % (h, first), align_bytes=64)
            nc.vector.quantize_mx(
                out=codes[:].bitcast(FP8X4), scales=plane[:], in_=source[:].rearrange("p w j -> p (w j)")
            )
            for b in range(width // P):
                h_codes[h, first + b] = codes[:, b * P : (b + 1) * P]
                h_bytes[h, first + b] = plane[:, b * P : (b + 1) * P]

        def multiply_unit(h, b):
            banks[h, b] = psum.tile([P, S], F32, name="bank%d%d" % (h, b))
            nc.tensor.matmul_mx(
                out=banks[h, b][:],
                lhsT=h_codes[h, b].bitcast(FP8X4),
                lhsT_scale=h_bytes[h, b],
                rhs=x_codes[:].bitcast(FP8X4),
                rhs_scale=x_bytes[:],
                start=True,
                stop=True,
            )

        def leave_psum(h, b):
            neg_scores[h, b] = placed("neg_scores", (h, b), [P, S], F32, score_offset)
            nc.vector.tensor_scalar(
                neg_scores[h, b][:], banks[h, b][:], -1.0, None, ALU.mult, ALU.min, accum_out=neg_max(h, b)
            )

        def row_sums(h, b):
            unused = sb.tile([P, S], BF16, name="spent%d%d" % (h, b))
            column = b * HEADS + h
            nc.scalar.activation(
                unused[:], neg_scores[h, b][:], ACT.Exp, bias=neg_max(h, b), scale=-1.0,
                accum_out=sums[:, column : column + 1],
            )

        def fetch(h, b, span):
            key = (h, b, span.start)
            neg_total[key] = placed("neg_total", key, [P, span.stop - span.start], F32, total_offset)
            window = neg_scores[h, b][:].indirect(paths[h][:, span.start // 16 : span.stop // 16])
            if h == 0:
                nc.scalar.activation(neg_total[key][:], window, ACT.Copy)
            else:
                nc.vector.tensor_tensor(neg_total[key][:], window, neg_total[h - 1, b, span.start][:], ALU.add)

        nc.vector.tensor_copy(x_bytes[:], table_scales[:].indirect(picks[:]))
        nc.vector.tensor_copy(x_codes[:], table_words[:].indirect(picks[:]))
        for h in (0, 1):
            for b in range(BLOCKS):
                if h == 1:
                    grouped[h, b] = reused.tile(
                        [P, P, PACK], BF16, name="grouped%d%d" % (h, b), offset=(20 + b) * KIB, align_bytes=64
                    )
                else:
                    grouped[h, b] = sb.tile([P, P, PACK], BF16, name="grouped%d%d" % (h, b), align_bytes=64)
                cast(grouped[h, b][:], raw[h, b], nc.vector.tensor_copy if (h, b) == (1, 1) else nc.scalar.copy)
                if h == 0:
                    quantise(h, b, grouped[h, b])
                    multiply_unit(h, b)
        for b in (1, 0):
            quantise(1, b, grouped[1, b])
            multiply_unit(1, b)
        for b in range(BLOCKS):
            leave_psum(0, b)
        last = reused.tile([P, V, PACK], BF16, name="grouped2", offset=20 * KIB, align_bytes=64)
        cast(last[:, 0:P, :], raw[2, 0], nc.scalar.copy)
        nc.gpsimd.tensor_scalar(last[:, P:V, :], raw[2, 1].rearrange("p j w -> p w j"), 1.0, 0.0, ALU.mult, ALU.add)
        quantise(2, 0, last)
        for b in range(BLOCKS):
            multiply_unit(2, b)
        for h, b in ((1, 1), (1, 0), (2, 0), (2, 1)):
            leave_psum(h, b)
        whole = slice(0, U)
        halves = [slice(c, c + U // 2) for c in range(0, U, U // 2)]
        for h in range(HEADS):
            for b in (1, 0) if h == 1 else (0, 1):
                row_sums(h, b)
            if h == 0:
                fetch(0, 0, whole)
            if h == 1:
                fetch(0, 1, halves[0])
        fetch(1, 0, whole)
        fetch(0, 1, halves[1])
        fetch(1, 1, halves[0])
        fetch(2, 0, whole)
        nc.vector.tensor_copy(max_term(HEADS - 1, BLOCKS - 1), last_low[:])

        product = reused.tile([P, BLOCKS], F32, name="product", offset=26 * KIB)
        nc.vector.tensor_reduce(product[:], sums[:].rearrange("p (b h) -> p b h", h=HEADS), AXIS.X, ALU.mult)
        pairs = factors[:].rearrange("p (b s) -> p b s", s=STEPS)[:, :, 1:GUESS_STEP]
        copies = [P, BLOCKS, DEGREE]
        bits = product[:].bitcast(U32)
        nc.scalar.activation(
            pairs[:, :, 1::2], bits.unsqueeze(2).to_broadcast(copies), ACT.Exp, bias=BIT_ZERO, scale=-BIT_STEP
        )
        nc.scalar.activation(pairs[:, :, 0::2], product[:].unsqueeze(2).to_broadcast(copies), ACT.Copy)
        nc.scalar.activation(terms[:, GUESS_STEP::STEPS], bits, ACT.Identity, bias=BIT_ZERO, scale=-BIT_STEP)
        fetch(2, 1, halves[0])
        fetch(1, 1, halves[1])
        running = sb.tile([P, BLOCKS * STEPS], F32, name="running")
        nc.vector.tensor_tensor_scan(running[:], factors[:], terms[:], 0.0, ALU.mult, ALU.add)
        fetch(2, 1, halves[1])
        for b, span in ((1, halves[0]), (0, whole), (1, halves[1])):
            result = sb.tile([P, span.stop - span.start], F32, name="result%d_%d" % (b, span.start))
            column = b * STEPS + LAST_STEP
            nc.scalar.activation(
                result[:], neg_total[HEADS - 1, b, span.start][:], ACT.Exp,
                bias=running[:, column : column + 1], scale=-1.0 / HEADS,
            )
            nc.sync.dma_start(out=out[b * P : (b + 1) * P, span], in_=result[:])
